import numpy as np, ml_dtypes
CORES = [51,54,179,182]
N = 4
import mx_ref
NC = 128
BF = ml_dtypes.bfloat16
def cut(t, i, w=512):
    return t[:, w * i:w * i + w]
def term(a, B):
    return np.stack([mx_ref.matmul(mx_ref.quantize(cut(a, i)), B) for i in range(4)], axis=2).reshape(128, -1)
def setup_inputs(rng):
    def f(*shape):
        return mx_ref.flush((rng.standard_normal(shape, dtype=np.float32) * np.exp2(rng.integers(-2, 3, shape[:-1] + (1,)))).astype(BF))
    return {"a": f(N, 128, 4 * 512), "b": f(N, 128, N * 4 * NC)}
def setup_inputs_blocks(rng):
    d = setup_inputs(rng)
    for k in ("a", "b"): d[k] = mx_ref.spread(d[k], rng, 2)
    return d
def setup_inputs_wide(rng):
    d = setup_inputs(rng)
    for k in ("a", "b"): d[k] = mx_ref.flush((d[k].astype(np.float32) * np.exp2(rng.integers(-4, 5, (N, 1, 1))).astype(np.float32)).astype(BF))
    return d
def setup_inputs_lossless(rng):
    a = np.zeros((N, 128, 4 * 128, 4), np.float32)
    for r in range(N):
        k = rng.integers(0, 512, size=4 * 128)
        a[r, k // 4, np.arange(4 * 128), k % 4] = 1.0
    size = np.repeat(2.0 ** rng.integers(-4, 5, size=(1, 1, (N * 4 * NC) // 4)), 4, axis=2)
    b = rng.integers(-1, 2, size=(N, 128, N * 4 * NC)) * size
    return {"a": a.reshape(N, 128, 4 * 512).astype(BF), "b": b.astype(np.float32).astype(BF)}
def reference(a, b):
    y = np.zeros((N, 128, 4 * NC), np.float32)
    for c in range(N):
        y[c] = mx_ref.total([term(a[r], mx_ref.quantize(cut(b[r], c, 4 * NC))) for r in range(N)])
    return {"y": y}

@@ -1,0 +1,167 @@
+from concourse.mybir import dt, AluOpType, ActivationFunctionType
+
+NT = 128
+NE = 4 * NT
+BANK = 512
+
+SCRATCH = {
+    "a_sb": ("sbuf", [128, 4 * NE], "bfloat16"),
+    "b_sb": ("sbuf", [128, 4 * NE], "bfloat16"),
+    "a_q": ("sbuf", [128, 4 * NT], "float8_e4m3fn_x4"),
+    "a_s": ("sbuf", [128, 4 * NT], "uint8"),
+    "b_q": ("sbuf", [128, 4 * NT], "float8_e4m3fn_x4"),
+    "b_s": ("sbuf", [128, 4 * NT], "uint8"),
+    "eye": ("sbuf", [128, NT], "bfloat16"),
+    "dia": ("sbuf", [128, NE + 8], "bfloat16"),
+    "s_q": ("sbuf", [128, 4 * NT], "float8_e4m3fn_x4"),
+    "s_s": ("sbuf", [128, 4 * NT], "uint8"),
+    "t_sb": ("sbuf", [128, 3 * NE], "bfloat16"),
+    "t_q": ("sbuf", [128, 3 * NT], "float8_e4m3fn_x4"),
+    "t_s": ("sbuf", [128, 3 * NT], "uint8"),
+    "l_q": ("sbuf", [128, 3 * NT], "float8_e4m3fn_x4"),
+    "l_s": ("sbuf", [128, 3 * NT], "uint8"),
+    "y_sb": ("sbuf", [128, NE], "float32"),
+    "ps": ("psum", [128, 8 * BANK], "float32"),
+}
+
+SEMAPHORES = (
+    ["ld_bx", "ld_a", "ld_bm", "ld_bl", "one", "zer", "eye", "dia", "qs", "qbx", "qbm", "qbl",
+     "c1", "c2", "c3", "c4", "qt1", "qt2", "qt3", "arr1", "arr2", "arr3", "sent", "stored"]
+    + ["qa%d" % i for i in range(4)]
+    + ["%s_%d" % (k, i) for k in ("m1", "m3", "u2", "u4") for i in range(4)]
+)
+
+
+def _bits(mask):
+    return [e for e in range(mask.bit_length()) if (mask >> e) & 1]
+
+
+def _mask_of(engines):
+    m = 0
+    for e in engines:
+        m |= 1 << e
+    return m
+
+
+def rank_program(g, core, T, topo):
+    rank = T.rank_of(core)
+    if rank is None:
+        return
+    V, S, PE, SY, sem = g.vector, g.scalar, g.tensor, g.sync, T.sem
+    Copy = ActivationFunctionType.Copy
+
+    others = [c for c in T.cores if c != core]
+    partner = [c for c in others if topo.host(c) == topo.host(core) and topo.chip(c) == topo.chip(core)][0]
+    far = [c for c in others if c != partner]
+    mine = [c for c in far if topo.die(c) == topo.die(core)][0]
+    his = [c for c in far if c != mine][0]
+    co, cp, cm, cx = rank, T.rank_of(partner), T.rank_of(mine), T.rank_of(his)
+
+    out_eng = _bits(topo.mask(core, mine))
+    chip_eng = _bits(topo.mask(core, partner))
+    side_eng = [e for e in chip_eng if e not in out_eng][:len(out_eng)] or out_eng
+    m_chain, n_chain = _mask_of(out_eng), len(out_eng)
+    m_side, n_side = _mask_of(side_eng), len(side_eng)
+
+    def el(c, n=1):
+        return slice(NE * c, NE * (c + n))
+
+    def wd(c, n=1):
+        return slice(NT * c, NT * (c + n))
+
+    def bank(k):
+        return T.ps[:, BANK * k:BANK * k + NT]
+
+    def mm(k, lq, ls, i, rq, rs, c, start, stop):
+        return PE.matmul_mx(bank(k), lq[:, wd(i)], ls[:, wd(i)], rq[:, wd(c)], rs[:, wd(c)], start, stop)
+
+    def send(slot, dst, land, mask, arr):
+        rid, pid = topo.addr(dst, core)
+        g.remote_dma(T.l_q[:, wd(land)].bitcast(dt.uint8), T.t_q[:, wd(slot)].bitcast(dt.uint8), arr, sem.sent, pid, rid, mask)
+        g.remote_dma(T.l_s[:, wd(land)], T.t_s[:, wd(slot)], arr, sem.sent, pid, rid, mask)
+
+    SY.dma_start(T.b_sb[:, el(cx)], T.b[:, el(cx)]).then_inc(sem.ld_bx, 16)
+    S.dma_start(T.a_sb[:], T.a[:, :]).then_inc(sem.ld_a, 16)
+    SY.dma_start(T.b_sb[:, el(cm)], T.b[:, el(cm)]).then_inc(sem.ld_bm, 16)
+    lo = min(co, cp)
+    SY.dma_start(T.b_sb[:, el(lo, 2)], T.b[:, el(lo, 2)]).then_inc(sem.ld_bl, 16)
+
+    V.memset(T.eye[:], 1.0).then_inc(sem.one, 1)
+    V.memset(T.dia[:], 0.0).then_inc(sem.zer, 1)
+    g.wait_ge(sem.one, 1)
+    g.affine_select(T.eye[:], T.eye[:], [[-1, NT]], AluOpType.is_equal, 0.0, 0, 1).then_inc(sem.eye, 1)
+    V.wait_ge(sem.zer, 1)
+    V.wait_ge(sem.eye, 1)
+    V.tensor_copy(T.dia[:, 3:NE:4], T.eye[:]).then_inc(sem.dia, 1)
+    V.wait_ge(sem.dia, 1)
+    for t in range(4):
+        V.quantize_mx(T.s_q[:, wd(t)], T.s_s[:, wd(t)], T.dia[:, 3 - t:3 - t + NE]).then_inc(sem.qs, 1)
+
+    V.wait_ge(sem.ld_bx, 16)
+    V.quantize_mx(T.b_q[:, wd(cx)], T.b_s[:, wd(cx)], T.b_sb[:, el(cx)]).then_inc(sem.qbx, 1)
+    V.wait_ge(sem.ld_a, 16)
+    PE.wait_ge(sem.qbx, 1)
+    for i in range(4):
+        V.quantize_mx(T.a_q[:, wd(i)], T.a_s[:, wd(i)], T.a_sb[:, el(i)]).then_inc(sem["qa%d" % i], 1)
+        PE.wait_ge(sem["qa%d" % i], 1)
+        mm(i, T.a_q, T.a_s, i, T.b_q, T.b_s, cx, True, True).then_inc(sem["m1_%d" % i], 1)
+
+    def drain(tag, banks, out, step_base, done, on_vector):
+        for i in range(4):
+            q = V if i in on_vector else S
+            q.wait_ge(sem["%s_%d" % (tag, i)], 1)
+            dst = out[:, step_base + i:step_base + NE:4]
+            if i in on_vector:
+                V.tensor_copy(dst, bank(banks + i)).then_inc(done, 1)
+            else:
+                S.activation(dst, bank(banks + i), Copy).then_inc(done, 1)
+
+    def pack(slot, done, ready):
+        V.wait_ge(done, 4)
+        V.quantize_mx(T.t_q[:, wd(slot)], T.t_s[:, wd(slot)], T.t_sb[:, el(slot)]).then_inc(ready, 1)
+
+    drain("m1", 0, T.t_sb, NE * 0, sem.c1, (3,))
+    pack(0, sem.c1, sem.qt1)
+    g.wait_ge(sem.qt1, 1)
+    send(0, partner, 0, m_chain, sem.arr1)
+
+    V.wait_ge(sem.ld_bm, 16)
+    V.quantize_mx(T.b_q[:, wd(cm)], T.b_s[:, wd(cm)], T.b_sb[:, el(cm)]).then_inc(sem.qbm, 1)
+    PE.wait_ge(sem.qbm, 1)
+    for i in range(4):
+        mm(4 + i, T.a_q, T.a_s, i, T.b_q, T.b_s, cm, True, False)
+
+    V.wait_ge(sem.ld_bl, 16)
+    V.quantize_mx(T.b_q[:, wd(lo, 2)], T.b_s[:, wd(lo, 2)], T.b_sb[:, el(lo, 2)]).then_inc(sem.qbl, 1)
+    PE.wait_ge(sem.qbl, 1)
+    PE.wait_ge(sem.c1, 4)
+    for i in range(4):
+        mm(i, T.a_q, T.a_s, i, T.b_q, T.b_s, cp, True, True).then_inc(sem["m3_%d" % i], 1)
+    drain("m3", 0, T.t_sb, NE * 1, sem.c3, (1, 3))
+    pack(1, sem.c3, sem.qt3)
+    g.wait_ge(sem.qt3, 1)
+    send(1, partner, 1, m_side, sem.arr2)
+
+    PE.wait_ge(sem.qs, 4)
+    PE.wait_ge(sem.arr1, 2 * n_chain)
+    for i in range(4):
+        mm(4 + i, T.s_q, T.s_s, i, T.l_q, T.l_s, 0, False, True).then_inc(sem["u2_%d" % i], 1)
+    drain("u2", 4, T.t_sb, NE * 2, sem.c2, (1, 3))
+    pack(2, sem.c2, sem.qt2)
+    g.wait_ge(sem.qt2, 1)
+    send(2, mine, 2, m_chain, sem.arr3)
+
+    PE.wait_ge(sem.c3, 4)
+    for i in range(4):
+        mm(i, T.a_q, T.a_s, i, T.b_q, T.b_s, co, True, False)
+    PE.wait_ge(sem.arr2, 2 * n_side)
+    for i in range(4):
+        mm(i, T.s_q, T.s_s, i, T.l_q, T.l_s, 1, False, False)
+    PE.wait_ge(sem.arr3, 2 * n_chain)
+    for i in range(4):
+        mm(i, T.s_q, T.s_s, i, T.l_q, T.l_s, 2, False, True).then_inc(sem["u4_%d" % i], 1)
+    drain("u4", 0, T.y_sb, 0, sem.c4, (1, 3))
+    SY.wait_ge(sem.c4, 4)
+    SY.dma_start(T.y[:, :], T.y_sb[:]).then_inc(sem.stored, 16)
+    SY.wait_ge(sem.stored, 16)
+    g.wait_ge(sem.sent, 4 * n_chain + 2 * n_side)

@@ -15,20 +15,23 @@ SCRATCH = {
     "dia": ("sbuf", [128, NE + 8], "bfloat16"),
     "s_q": ("sbuf", [128, 4 * NT], "float8_e4m3fn_x4"),
     "s_s": ("sbuf", [128, 4 * NT], "uint8"),
-    "t_sb": ("sbuf", [128, 3 * NE], "bfloat16"),
-    "t_q": ("sbuf", [128, 3 * NT], "float8_e4m3fn_x4"),
-    "t_s": ("sbuf", [128, 3 * NT], "uint8"),
-    "l_q": ("sbuf", [128, 3 * NT], "float8_e4m3fn_x4"),
-    "l_s": ("sbuf", [128, 3 * NT], "uint8"),
+    "t_sb": ("sbuf", [128, NE], "bfloat16"),
+    "t_q": ("sbuf", [128, NT], "float8_e4m3fn_x4"),
+    "t_s": ("sbuf", [128, NT], "uint8"),
+    "pa_q": ("sbuf", [128, 4 * NT], "float8_e4m3fn_x4"),
+    "pa_s": ("sbuf", [128, 4 * NT], "uint8"),
+    "pb_q": ("sbuf", [128, 2 * NT], "float8_e4m3fn_x4"),
+    "pb_s": ("sbuf", [128, 2 * NT], "uint8"),
+    "f_q": ("sbuf", [128, NT], "float8_e4m3fn_x4"),
+    "f_s": ("sbuf", [128, NT], "uint8"),
     "y_sb": ("sbuf", [128, NE], "float32"),
     "ps": ("psum", [128, 8 * BANK], "float32"),
 }
 
 SEMAPHORES = (
-    ["ld_bx", "ld_a", "ld_bm", "ld_bl", "one", "zer", "eye", "dia", "qs", "qbx", "qbm", "qbl",
-     "c1", "c2", "c3", "c4", "qt1", "qt2", "qt3", "arr1", "arr2", "arr3", "sent", "stored"]
-    + ["qa%d" % i for i in range(4)]
-    + ["%s_%d" % (k, i) for k in ("m1", "m3", "u2", "u4") for i in range(4)]
+    ["ld_bx", "ld_a0", "ld_a1", "ld_bm", "ld_bl", "one", "zer", "eye", "dia", "qs", "qbx", "qa0", "qa1", "qbm", "qbl",
+     "c2", "c4", "qt2", "arr_bx", "arr_a0", "arr_a1", "arr_bp", "arr_f", "sent", "stored"]
+    + ["%s_%d" % (k, i) for k in ("u2", "u4") for i in range(4)]
 )
 
 
@@ -59,9 +62,9 @@ def rank_program(g, core, T, topo):
 
     out_eng = _bits(topo.mask(core, mine))
     chip_eng = _bits(topo.mask(core, partner))
-    side_eng = [e for e in chip_eng if e not in out_eng][:len(out_eng)] or out_eng
-    m_chain, n_chain = _mask_of(out_eng), len(out_eng)
-    m_side, n_side = _mask_of(side_eng), len(side_eng)
+    side_eng = [e for e in chip_eng if e not in out_eng] or chip_eng
+    OUT, CHIP, SIDE = [(_mask_of(e), len(e)) for e in (out_eng, chip_eng, side_eng)]
+    total = [0]
 
     def el(c, n=1):
         return slice(NE * c, NE * (c + n))
@@ -75,15 +78,20 @@ def rank_program(g, core, T, topo):
     def mm(k, lq, ls, i, rq, rs, c, start, stop):
         return PE.matmul_mx(bank(k), lq[:, wd(i)], ls[:, wd(i)], rq[:, wd(c)], rs[:, wd(c)], start, stop)
 
-    def send(slot, dst, land, mask, arr):
+    def send(dst, dq, ds, dcols, sq, ss, scols, eng, arr):
         rid, pid = topo.addr(dst, core)
-        g.remote_dma(T.l_q[:, wd(land)].bitcast(dt.uint8), T.t_q[:, wd(slot)].bitcast(dt.uint8), arr, sem.sent, pid, rid, mask)
-        g.remote_dma(T.l_s[:, wd(land)], T.t_s[:, wd(slot)], arr, sem.sent, pid, rid, mask)
+        g.remote_dma(dq[:, dcols].bitcast(dt.uint8), sq[:, scols].bitcast(dt.uint8), arr, sem.sent, pid, rid, eng[0])
+        g.remote_dma(ds[:, dcols], ss[:, scols], arr, sem.sent, pid, rid, eng[0])
+        total[0] += 2 * eng[1]
 
-    SY.dma_start(T.b_sb[:, el(cx)], T.b[:, el(cx)]).then_inc(sem.ld_bx, 16)
-    S.dma_start(T.a_sb[:], T.a[:, :]).then_inc(sem.ld_a, 16)
-    SY.dma_start(T.b_sb[:, el(cm)], T.b[:, el(cm)]).then_inc(sem.ld_bm, 16)
+    def quant(q, s, src, c, n, ready):
+        V.quantize_mx(q[:, wd(c, n)], s[:, wd(c, n)], src[:, el(c, n)]).then_inc(ready, 1)
+
     lo = min(co, cp)
+    SY.dma_start(T.b_sb[:, el(cx)], T.b[:, el(cx)]).then_inc(sem.ld_bx, 16)
+    S.dma_start(T.a_sb[:, el(0, 2)], T.a[:, el(0, 2)]).then_inc(sem.ld_a0, 16)
+    SY.dma_start(T.a_sb[:, el(2, 2)], T.a[:, el(2, 2)]).then_inc(sem.ld_a1, 16)
+    SY.dma_start(T.b_sb[:, el(cm)], T.b[:, el(cm)]).then_inc(sem.ld_bm, 16)
     SY.dma_start(T.b_sb[:, el(lo, 2)], T.b[:, el(lo, 2)]).then_inc(sem.ld_bl, 16)
 
     V.memset(T.eye[:], 1.0).then_inc(sem.one, 1)
@@ -98,70 +106,58 @@ def rank_program(g, core, T, topo):
         V.quantize_mx(T.s_q[:, wd(t)], T.s_s[:, wd(t)], T.dia[:, 3 - t:3 - t + NE]).then_inc(sem.qs, 1)
 
     V.wait_ge(sem.ld_bx, 16)
-    V.quantize_mx(T.b_q[:, wd(cx)], T.b_s[:, wd(cx)], T.b_sb[:, el(cx)]).then_inc(sem.qbx, 1)
-    V.wait_ge(sem.ld_a, 16)
-    PE.wait_ge(sem.qbx, 1)
-    for i in range(4):
-        V.quantize_mx(T.a_q[:, wd(i)], T.a_s[:, wd(i)], T.a_sb[:, el(i)]).then_inc(sem["qa%d" % i], 1)
-        PE.wait_ge(sem["qa%d" % i], 1)
-        mm(i, T.a_q, T.a_s, i, T.b_q, T.b_s, cx, True, True).then_inc(sem["m1_%d" % i], 1)
+    quant(T.b_q, T.b_s, T.b_sb, cx, 1, sem.qbx)
+    g.wait_ge(sem.qbx, 1)
+    send(partner, T.pb_q, T.pb_s, wd(0), T.b_q, T.b_s, wd(cx), CHIP, sem.arr_bx)
+    for h in range(2):
+        V.wait_ge(sem["ld_a%d" % h], 16)
+        quant(T.a_q, T.a_s, T.a_sb, 2 * h, 2, sem["qa%d" % h])
+        g.wait_ge(sem["qa%d" % h], 1)
+        send(partner, T.pa_q, T.pa_s, wd(2 * h, 2), T.a_q, T.a_s, wd(2 * h, 2), CHIP, sem["arr_a%d" % h])
+    V.wait_ge(sem.ld_bm, 16)
+    quant(T.b_q, T.b_s, T.b_sb, cm, 1, sem.qbm)
+    V.wait_ge(sem.ld_bl, 16)
+    quant(T.b_q, T.b_s, T.b_sb, lo, 2, sem.qbl)
+    g.wait_ge(sem.qbl, 1)
+    send(partner, T.pb_q, T.pb_s, wd(1), T.b_q, T.b_s, wd(cp), SIDE, sem.arr_bp)
 
-    def drain(tag, banks, out, step_base, done, on_vector):
+    def drain(tag, banks, out, done, on_vector):
         for i in range(4):
             q = V if i in on_vector else S
             q.wait_ge(sem["%s_%d" % (tag, i)], 1)
-            dst = out[:, step_base + i:step_base + NE:4]
             if i in on_vector:
-                V.tensor_copy(dst, bank(banks + i)).then_inc(done, 1)
+                V.tensor_copy(out[:, i:NE:4], bank(banks + i)).then_inc(done, 1)
             else:
-                S.activation(dst, bank(banks + i), Copy).then_inc(done, 1)
+                S.activation(out[:, i:NE:4], bank(banks + i), Copy).then_inc(done, 1)
 
-    def pack(slot, done, ready):
-        V.wait_ge(done, 4)
-        V.quantize_mx(T.t_q[:, wd(slot)], T.t_s[:, wd(slot)], T.t_sb[:, el(slot)]).then_inc(ready, 1)
-
-    drain("m1", 0, T.t_sb, NE * 0, sem.c1, (3,))
-    pack(0, sem.c1, sem.qt1)
-    g.wait_ge(sem.qt1, 1)
-    send(0, partner, 0, m_chain, sem.arr1)
-
-    V.wait_ge(sem.ld_bm, 16)
-    V.quantize_mx(T.b_q[:, wd(cm)], T.b_s[:, wd(cm)], T.b_sb[:, el(cm)]).then_inc(sem.qbm, 1)
+    PE.wait_ge(sem.qa0, 1)
+    PE.wait_ge(sem.qa1, 1)
     PE.wait_ge(sem.qbm, 1)
     for i in range(4):
         mm(4 + i, T.a_q, T.a_s, i, T.b_q, T.b_s, cm, True, False)
-
-    V.wait_ge(sem.ld_bl, 16)
-    V.quantize_mx(T.b_q[:, wd(lo, 2)], T.b_s[:, wd(lo, 2)], T.b_sb[:, el(lo, 2)]).then_inc(sem.qbl, 1)
-    PE.wait_ge(sem.qbl, 1)
-    PE.wait_ge(sem.c1, 4)
+    PE.wait_ge(sem.arr_bx, 2 * CHIP[1])
     for i in range(4):
-        mm(i, T.a_q, T.a_s, i, T.b_q, T.b_s, cp, True, True).then_inc(sem["m3_%d" % i], 1)
-    drain("m3", 0, T.t_sb, NE * 1, sem.c3, (1, 3))
-    pack(1, sem.c3, sem.qt3)
-    g.wait_ge(sem.qt3, 1)
-    send(1, partner, 1, m_side, sem.arr2)
-
-    PE.wait_ge(sem.qs, 4)
-    PE.wait_ge(sem.arr1, 2 * n_chain)
-    for i in range(4):
-        mm(4 + i, T.s_q, T.s_s, i, T.l_q, T.l_s, 0, False, True).then_inc(sem["u2_%d" % i], 1)
-    drain("u2", 4, T.t_sb, NE * 2, sem.c2, (1, 3))
-    pack(2, sem.c2, sem.qt2)
+        if i % 2 == 0:
+            PE.wait_ge(sem["arr_a%d" % (i // 2)], 2 * CHIP[1])
+        mm(4 + i, T.pa_q, T.pa_s, i, T.pb_q, T.pb_s, 0, False, True).then_inc(sem["u2_%d" % i], 1)
+    drain("u2", 4, T.t_sb, sem.c2, (3,))
+    V.wait_ge(sem.c2, 4)
+    V.quantize_mx(T.t_q[:], T.t_s[:], T.t_sb[:]).then_inc(sem.qt2, 1)
     g.wait_ge(sem.qt2, 1)
-    send(2, mine, 2, m_chain, sem.arr3)
+    send(mine, T.f_q, T.f_s, wd(0), T.t_q, T.t_s, wd(0), OUT, sem.arr_f)
 
-    PE.wait_ge(sem.c3, 4)
+    PE.wait_ge(sem.qbl, 1)
     for i in range(4):
         mm(i, T.a_q, T.a_s, i, T.b_q, T.b_s, co, True, False)
-    PE.wait_ge(sem.arr2, 2 * n_side)
+    PE.wait_ge(sem.arr_bp, 2 * SIDE[1])
     for i in range(4):
-        mm(i, T.s_q, T.s_s, i, T.l_q, T.l_s, 1, False, False)
-    PE.wait_ge(sem.arr3, 2 * n_chain)
+        mm(i, T.pa_q, T.pa_s, i, T.pb_q, T.pb_s, 1, False, False)
+    PE.wait_ge(sem.qs, 4)
+    PE.wait_ge(sem.arr_f, 2 * OUT[1])
     for i in range(4):
-        mm(i, T.s_q, T.s_s, i, T.l_q, T.l_s, 2, False, True).then_inc(sem["u4_%d" % i], 1)
-    drain("u4", 0, T.y_sb, 0, sem.c4, (1, 3))
+        mm(i, T.s_q, T.s_s, i, T.f_q, T.f_s, 0, False, True).then_inc(sem["u4_%d" % i], 1)
+    drain("u4", 0, T.y_sb, sem.c4, (1, 3))
     SY.wait_ge(sem.c4, 4)
     SY.dma_start(T.y[:, :], T.y_sb[:]).then_inc(sem.stored, 16)
     SY.wait_ge(sem.stored, 16)
-    g.wait_ge(sem.sent, 4 * n_chain + 2 * n_side)
+    g.wait_ge(sem.sent, total[0])

@@ -1,6 +1,7 @@
 from concourse.mybir import dt, AluOpType, ActivationFunctionType
 
 NT = 128
+NH = NT // 2
 NE = 4 * NT
 BANK = 512
 
@@ -15,23 +16,30 @@ SCRATCH = {
     "dia": ("sbuf", [128, NE + 8], "bfloat16"),
     "s_q": ("sbuf", [128, 4 * NT], "float8_e4m3fn_x4"),
     "s_s": ("sbuf", [128, 4 * NT], "uint8"),
+    "z_sb": ("sbuf", [128, NE], "bfloat16"),
     "t_sb": ("sbuf", [128, NE], "bfloat16"),
     "t_q": ("sbuf", [128, NT], "float8_e4m3fn_x4"),
     "t_s": ("sbuf", [128, NT], "uint8"),
+    "h_sb": ("sbuf", [128, NE], "bfloat16"),
+    "h_q": ("sbuf", [128, NT], "float8_e4m3fn_x4"),
+    "h_s": ("sbuf", [128, NT], "uint8"),
     "pa_q": ("sbuf", [128, 4 * NT], "float8_e4m3fn_x4"),
     "pa_s": ("sbuf", [128, 4 * NT], "uint8"),
     "pb_q": ("sbuf", [128, 2 * NT], "float8_e4m3fn_x4"),
     "pb_s": ("sbuf", [128, 2 * NT], "uint8"),
     "f_q": ("sbuf", [128, NT], "float8_e4m3fn_x4"),
     "f_s": ("sbuf", [128, NT], "uint8"),
+    "r_q": ("sbuf", [128, 2 * NT + NH], "float8_e4m3fn_x4"),
+    "r_s": ("sbuf", [128, 2 * NT + NH], "uint8"),
     "y_sb": ("sbuf", [128, NE], "float32"),
     "ps": ("psum", [128, 8 * BANK], "float32"),
 }
 
 SEMAPHORES = (
-    ["ld_bx", "ld_a0", "ld_a1", "ld_bm", "ld_bl", "one", "zer", "eye", "dia", "qs", "qbx", "qa0", "qa1", "qbm", "qbl",
-     "c2", "c4", "qt2", "arr_bx", "arr_a0", "arr_a1", "arr_bp", "arr_f", "sent", "stored"]
-    + ["%s_%d" % (k, i) for k in ("u2", "u4") for i in range(4)]
+    ["ld_bx", "ld_a0", "ld_a1", "ld_bm", "ld_bp", "ld_bo", "one", "zer", "zz", "eye", "dia", "qs", "qz",
+     "qbx", "qa0", "qa1", "qbm", "qbp", "qbo", "ch", "ct", "c4", "qh", "qt",
+     "arr_bx", "arr_a0", "arr_a1", "arr_bp", "arr_f", "arr_h", "sent", "stored"]
+    + ["ud_%d" % q for q in range(2)] + ["up_%d" % q for q in range(2)] + ["uy_%d" % i for i in range(4)]
 )
 
 
@@ -59,8 +67,9 @@ def rank_program(g, core, T, topo):
     mine = [c for c in far if topo.die(c) == topo.die(core)][0]
     his = [c for c in far if c != mine][0]
     co, cp, cm, cx = rank, T.rank_of(partner), T.rank_of(mine), T.rank_of(his)
+    fl = min(cm, cx)
 
-    out_eng = _bits(topo.mask(core, mine))
+    out_eng = _bits(topo.mask(core, mine) & topo.mask(core, his))
     chip_eng = _bits(topo.mask(core, partner))
     side_eng = [e for e in chip_eng if e not in out_eng] or chip_eng
     OUT, CHIP, SIDE = [(_mask_of(e), len(e)) for e in (out_eng, chip_eng, side_eng)]
@@ -72,8 +81,8 @@ def rank_program(g, core, T, topo):
     def wd(c, n=1):
         return slice(NT * c, NT * (c + n))
 
-    def bank(k):
-        return T.ps[:, BANK * k:BANK * k + NT]
+    def bank(k, lo=0, n=NT):
+        return T.ps[:, BANK * k + lo:BANK * k + lo + n]
 
     def mm(k, lq, ls, i, rq, rs, c, start, stop):
         return PE.matmul_mx(bank(k), lq[:, wd(i)], ls[:, wd(i)], rq[:, wd(c)], rs[:, wd(c)], start, stop)
@@ -87,15 +96,23 @@ def rank_program(g, core, T, topo):
     def quant(q, s, src, c, n, ready):
         V.quantize_mx(q[:, wd(c, n)], s[:, wd(c, n)], src[:, el(c, n)]).then_inc(ready, 1)
 
-    lo = min(co, cp)
+    def cast(q, out, in_, done):
+        if q == 0:
+            V.tensor_copy(out, in_).then_inc(done, 1)
+        else:
+            S.activation(out, in_, Copy).then_inc(done, 1)
+
     SY.dma_start(T.b_sb[:, el(cx)], T.b[:, el(cx)]).then_inc(sem.ld_bx, 16)
     S.dma_start(T.a_sb[:, el(0, 2)], T.a[:, el(0, 2)]).then_inc(sem.ld_a0, 16)
     SY.dma_start(T.a_sb[:, el(2, 2)], T.a[:, el(2, 2)]).then_inc(sem.ld_a1, 16)
-    SY.dma_start(T.b_sb[:, el(cm)], T.b[:, el(cm)]).then_inc(sem.ld_bm, 16)
-    SY.dma_start(T.b_sb[:, el(lo, 2)], T.b[:, el(lo, 2)]).then_inc(sem.ld_bl, 16)
+    S.dma_start(T.b_sb[:, el(cm)], T.b[:, el(cm)]).then_inc(sem.ld_bm, 16)
+    SY.dma_start(T.b_sb[:, el(cp)], T.b[:, el(cp)]).then_inc(sem.ld_bp, 16)
+    S.dma_start(T.b_sb[:, el(co)], T.b[:, el(co)]).then_inc(sem.ld_bo, 16)
 
     V.memset(T.eye[:], 1.0).then_inc(sem.one, 1)
     V.memset(T.dia[:], 0.0).then_inc(sem.zer, 1)
+    V.memset(T.z_sb[:], 0.0).then_inc(sem.zz, 1)
+    V.memset(T.h_sb[:, NE // 2:NE], 0.0).then_inc(sem.zz, 1)
     g.wait_ge(sem.one, 1)
     g.affine_select(T.eye[:], T.eye[:], [[-1, NT]], AluOpType.is_equal, 0.0, 0, 1).then_inc(sem.eye, 1)
     V.wait_ge(sem.zer, 1)
@@ -109,54 +126,79 @@ def rank_program(g, core, T, topo):
     quant(T.b_q, T.b_s, T.b_sb, cx, 1, sem.qbx)
     g.wait_ge(sem.qbx, 1)
     send(partner, T.pb_q, T.pb_s, wd(0), T.b_q, T.b_s, wd(cx), CHIP, sem.arr_bx)
-    for h in range(2):
-        V.wait_ge(sem["ld_a%d" % h], 16)
-        quant(T.a_q, T.a_s, T.a_sb, 2 * h, 2, sem["qa%d" % h])
-        g.wait_ge(sem["qa%d" % h], 1)
-        send(partner, T.pa_q, T.pa_s, wd(2 * h, 2), T.a_q, T.a_s, wd(2 * h, 2), CHIP, sem["arr_a%d" % h])
+    V.wait_ge(sem.ld_a0, 16)
+    quant(T.a_q, T.a_s, T.a_sb, 0, 2, sem.qa0)
+    g.wait_ge(sem.qa0, 1)
+    send(partner, T.pa_q, T.pa_s, wd(0, 2), T.a_q, T.a_s, wd(0, 2), CHIP, sem.arr_a0)
+    V.wait_ge(sem.zz, 2)
+    for lo in (0, NT + NH):
+        V.quantize_mx(T.r_q[:, lo:lo + NT], T.r_s[:, lo:lo + NT], T.z_sb[:]).then_inc(sem.qz, 1)
+    V.wait_ge(sem.ld_a1, 16)
+    quant(T.a_q, T.a_s, T.a_sb, 2, 2, sem.qa1)
+    g.wait_ge(sem.qa1, 1)
+    send(partner, T.pa_q, T.pa_s, wd(2, 2), T.a_q, T.a_s, wd(2, 2), SIDE, sem.arr_a1)
     V.wait_ge(sem.ld_bm, 16)
     quant(T.b_q, T.b_s, T.b_sb, cm, 1, sem.qbm)
-    V.wait_ge(sem.ld_bl, 16)
-    quant(T.b_q, T.b_s, T.b_sb, lo, 2, sem.qbl)
-    g.wait_ge(sem.qbl, 1)
+    V.wait_ge(sem.ld_bp, 16)
+    quant(T.b_q, T.b_s, T.b_sb, cp, 1, sem.qbp)
+    g.wait_ge(sem.qbp, 1)
     send(partner, T.pb_q, T.pb_s, wd(1), T.b_q, T.b_s, wd(cp), SIDE, sem.arr_bp)
 
-    def drain(tag, banks, out, done, on_vector):
-        for i in range(4):
-            q = V if i in on_vector else S
-            q.wait_ge(sem["%s_%d" % (tag, i)], 1)
-            if i in on_vector:
-                V.tensor_copy(out[:, i:NE:4], bank(banks + i)).then_inc(done, 1)
-            else:
-                S.activation(out[:, i:NE:4], bank(banks + i), Copy).then_inc(done, 1)
-
-    PE.wait_ge(sem.qa0, 1)
     PE.wait_ge(sem.qa1, 1)
+    PE.wait_ge(sem.qbx, 1)
     PE.wait_ge(sem.qbm, 1)
-    for i in range(4):
-        mm(4 + i, T.a_q, T.a_s, i, T.b_q, T.b_s, cm, True, False)
+    for q in range(2):
+        PE.matmul_mx(bank(6 + q, 0, 2 * NT), T.a_q[:, wd(2 + q)], T.a_s[:, wd(2 + q)],
+                     T.b_q[:, wd(fl, 2)], T.b_s[:, wd(fl, 2)], True, True).then_inc(sem["ud_%d" % q], 1)
+    PE.wait_ge(sem.qa0, 1)
+    for q in range(2):
+        mm(4 + q, T.a_q, T.a_s, q, T.b_q, T.b_s, cm, True, False)
+    for q in range(2):
+        (V if q == 0 else S).wait_ge(sem["ud_%d" % q], 1)
+        for h in range(2):
+            cast(q, T.h_sb[:, 2 * h + q:NE // 2:4], bank(6 + q, NT * (cx - fl) + NH * h, NH), sem.ch)
+    V.wait_ge(sem.ch, 4)
+    V.quantize_mx(T.h_q[:], T.h_s[:], T.h_sb[:]).then_inc(sem.qh, 1)
+    g.wait_ge(sem.qh, 1)
+    send(his, T.r_q, T.r_s, slice(NT, NT + NH), T.h_q, T.h_s, slice(0, NH), OUT, sem.arr_h)
+    for q in range(2):
+        cast(q, T.t_sb[:, 2 + q:NE:4], bank(6 + q, NT * (cm - fl), NT), sem.ct)
+    V.wait_ge(sem.ld_bo, 16)
+    quant(T.b_q, T.b_s, T.b_sb, co, 1, sem.qbo)
+
     PE.wait_ge(sem.arr_bx, 2 * CHIP[1])
-    for i in range(4):
-        if i % 2 == 0:
-            PE.wait_ge(sem["arr_a%d" % (i // 2)], 2 * CHIP[1])
-        mm(4 + i, T.pa_q, T.pa_s, i, T.pb_q, T.pb_s, 0, False, True).then_inc(sem["u2_%d" % i], 1)
-    drain("u2", 4, T.t_sb, sem.c2, (3,))
-    V.wait_ge(sem.c2, 4)
-    V.quantize_mx(T.t_q[:], T.t_s[:], T.t_sb[:]).then_inc(sem.qt2, 1)
-    g.wait_ge(sem.qt2, 1)
+    PE.wait_ge(sem.arr_a0, 2 * CHIP[1])
+    for q in range(2):
+        mm(4 + q, T.pa_q, T.pa_s, q, T.pb_q, T.pb_s, 0, False, True).then_inc(sem["up_%d" % q], 1)
+    for q in range(2):
+        (V if q == 1 else S).wait_ge(sem["up_%d" % q], 1)
+        cast(1 - q, T.t_sb[:, q:NE:4], bank(4 + q), sem.ct)
+    V.wait_ge(sem.ct, 4)
+    V.quantize_mx(T.t_q[:], T.t_s[:], T.t_sb[:]).then_inc(sem.qt, 1)
+    g.wait_ge(sem.qt, 1)
     send(mine, T.f_q, T.f_s, wd(0), T.t_q, T.t_s, wd(0), OUT, sem.arr_f)
 
-    PE.wait_ge(sem.qbl, 1)
+    PE.wait_ge(sem.qbo, 1)
     for i in range(4):
         mm(i, T.a_q, T.a_s, i, T.b_q, T.b_s, co, True, False)
+    PE.wait_ge(sem.arr_a1, 2 * SIDE[1])
     PE.wait_ge(sem.arr_bp, 2 * SIDE[1])
     for i in range(4):
         mm(i, T.pa_q, T.pa_s, i, T.pb_q, T.pb_s, 1, False, False)
     PE.wait_ge(sem.qs, 4)
+    PE.wait_ge(sem.qz, 2)
+    PE.wait_ge(sem.arr_h, 2 * OUT[1])
+    for q in range(2):
+        for h in range(2):
+            v = slice(NT - NH * h, 2 * NT - NH * h)
+            PE.matmul_mx(bank(2 + q), T.s_q[:, wd(2 * h + q)], T.s_s[:, wd(2 * h + q)], T.r_q[:, v], T.r_s[:, v],
+                         False, False)
     PE.wait_ge(sem.arr_f, 2 * OUT[1])
     for i in range(4):
-        mm(i, T.s_q, T.s_s, i, T.f_q, T.f_s, 0, False, True).then_inc(sem["u4_%d" % i], 1)
-    drain("u4", 0, T.y_sb, sem.c4, (1, 3))
+        mm(i, T.s_q, T.s_s, i, T.f_q, T.f_s, 0, False, True).then_inc(sem["uy_%d" % i], 1)
+    for i in range(4):
+        (V if i % 2 == 1 else S).wait_ge(sem["uy_%d" % i], 1)
+        cast(1 - i % 2, T.y_sb[:, i:NE:4], bank(i), sem.c4)
     SY.wait_ge(sem.c4, 4)
     SY.dma_start(T.y[:, :], T.y_sb[:]).then_inc(sem.stored, 16)
     SY.wait_ge(sem.stored, 16)

@@ -5,28 +5,26 @@ NH = NT // 2
 NE = 4 * NT
 BANK = 512
 
+U_BM, U_BX, U_A, U_BP, U_BO = 0, 1, 2, 6, 7
+P_BX, P_A, P_BP = 0, 1, 5
+
 SCRATCH = {
     "a_sb": ("sbuf", [128, 4 * NE], "bfloat16"),
     "b_sb": ("sbuf", [128, 4 * NE], "bfloat16"),
-    "a_q": ("sbuf", [128, 4 * NT], "float8_e4m3fn_x4"),
-    "a_s": ("sbuf", [128, 4 * NT], "uint8"),
-    "b_q": ("sbuf", [128, 4 * NT], "float8_e4m3fn_x4"),
-    "b_s": ("sbuf", [128, 4 * NT], "uint8"),
+    "u_q": ("sbuf", [128, 8 * NT], "float8_e4m3fn_x4"),
+    "u_s": ("sbuf", [128, 8 * NT], "uint8"),
+    "p_q": ("sbuf", [128, 6 * NT], "float8_e4m3fn_x4"),
+    "p_s": ("sbuf", [128, 6 * NT], "uint8"),
     "eye": ("sbuf", [128, NT], "bfloat16"),
     "dia": ("sbuf", [128, NE + 8], "bfloat16"),
     "s_q": ("sbuf", [128, 4 * NT], "float8_e4m3fn_x4"),
     "s_s": ("sbuf", [128, 4 * NT], "uint8"),
-    "z_sb": ("sbuf", [128, NE], "bfloat16"),
     "t_sb": ("sbuf", [128, NE], "bfloat16"),
     "t_q": ("sbuf", [128, NT], "float8_e4m3fn_x4"),
     "t_s": ("sbuf", [128, NT], "uint8"),
     "h_sb": ("sbuf", [128, NE], "bfloat16"),
     "h_q": ("sbuf", [128, NT], "float8_e4m3fn_x4"),
     "h_s": ("sbuf", [128, NT], "uint8"),
-    "pa_q": ("sbuf", [128, 4 * NT], "float8_e4m3fn_x4"),
-    "pa_s": ("sbuf", [128, 4 * NT], "uint8"),
-    "pb_q": ("sbuf", [128, 2 * NT], "float8_e4m3fn_x4"),
-    "pb_s": ("sbuf", [128, 2 * NT], "uint8"),
     "f_q": ("sbuf", [128, NT], "float8_e4m3fn_x4"),
     "f_s": ("sbuf", [128, NT], "uint8"),
     "r_q": ("sbuf", [128, 2 * NT + NH], "float8_e4m3fn_x4"),
@@ -38,7 +36,7 @@ SCRATCH = {
 SEMAPHORES = (
     ["ld_bx", "ld_a0", "ld_a1", "ld_bm", "ld_bp", "ld_bo", "one", "zer", "zz", "eye", "dia", "qs", "qz",
      "qbx", "qa0", "qa1", "qbm", "qbp", "qbo", "ch", "ct", "c4", "qh", "qt",
-     "arr_bx", "arr_a0", "arr_a1", "arr_bp", "arr_f", "arr_h", "sent", "stored"]
+     "arr_1", "arr_2", "arr_f", "arr_h", "sent", "stored"]
     + ["ud_%d" % q for q in range(2)] + ["up_%d" % q for q in range(2)] + ["uy_%d" % i for i in range(4)]
 )
 
@@ -67,7 +65,6 @@ def rank_program(g, core, T, topo):
     mine = [c for c in far if topo.die(c) == topo.die(core)][0]
     his = [c for c in far if c != mine][0]
     co, cp, cm, cx = rank, T.rank_of(partner), T.rank_of(mine), T.rank_of(his)
-    fl = min(cm, cx)
 
     out_eng = _bits(topo.mask(core, mine) & topo.mask(core, his))
     chip_eng = _bits(topo.mask(core, partner))
@@ -87,14 +84,18 @@ def rank_program(g, core, T, topo):
     def mm(k, lq, ls, i, rq, rs, c, start, stop):
         return PE.matmul_mx(bank(k), lq[:, wd(i)], ls[:, wd(i)], rq[:, wd(c)], rs[:, wd(c)], start, stop)
 
-    def send(dst, dq, ds, dcols, sq, ss, scols, eng, arr):
+    def codes(dst, dq, dcols, sq, scols, eng, arr):
         rid, pid = topo.addr(dst, core)
         g.remote_dma(dq[:, dcols].bitcast(dt.uint8), sq[:, scols].bitcast(dt.uint8), arr, sem.sent, pid, rid, eng[0])
-        g.remote_dma(ds[:, dcols], ss[:, scols], arr, sem.sent, pid, rid, eng[0])
-        total[0] += 2 * eng[1]
+        total[0] += eng[1]
 
-    def quant(q, s, src, c, n, ready):
-        V.quantize_mx(q[:, wd(c, n)], s[:, wd(c, n)], src[:, el(c, n)]).then_inc(ready, 1)
+    def plane(dst, ds, dcols, ss, scols, eng, arr):
+        rid, pid = topo.addr(dst, core)
+        g.remote_dma(ds[:, dcols], ss[:, scols], arr, sem.sent, pid, rid, eng[0])
+        total[0] += eng[1]
+
+    def quant(u, src, c, n, ready):
+        V.quantize_mx(T.u_q[:, wd(u, n)], T.u_s[:, wd(u, n)], src[:, el(c, n)]).then_inc(ready, 1)
 
     def cast(q, out, in_, done):
         if q == 0:
@@ -110,81 +111,83 @@ def rank_program(g, core, T, topo):
     S.dma_start(T.b_sb[:, el(co)], T.b[:, el(co)]).then_inc(sem.ld_bo, 16)
 
     V.memset(T.eye[:], 1.0).then_inc(sem.one, 1)
-    V.memset(T.dia[:], 0.0).then_inc(sem.zer, 1)
-    V.memset(T.z_sb[:], 0.0).then_inc(sem.zz, 1)
     V.memset(T.h_sb[:, NE // 2:NE], 0.0).then_inc(sem.zz, 1)
+    V.memset(T.dia[:], 0.0).then_inc(sem.zer, 1)
     g.wait_ge(sem.one, 1)
     g.affine_select(T.eye[:], T.eye[:], [[-1, NT]], AluOpType.is_equal, 0.0, 0, 1).then_inc(sem.eye, 1)
-    V.wait_ge(sem.zer, 1)
-    V.wait_ge(sem.eye, 1)
-    V.tensor_copy(T.dia[:, 3:NE:4], T.eye[:]).then_inc(sem.dia, 1)
-    V.wait_ge(sem.dia, 1)
-    for t in range(4):
-        V.quantize_mx(T.s_q[:, wd(t)], T.s_s[:, wd(t)], T.dia[:, 3 - t:3 - t + NE]).then_inc(sem.qs, 1)
 
     V.wait_ge(sem.ld_bx, 16)
-    quant(T.b_q, T.b_s, T.b_sb, cx, 1, sem.qbx)
+    quant(U_BX, T.b_sb, cx, 1, sem.qbx)
     g.wait_ge(sem.qbx, 1)
-    send(partner, T.pb_q, T.pb_s, wd(0), T.b_q, T.b_s, wd(cx), CHIP, sem.arr_bx)
+    codes(partner, T.p_q, wd(P_BX), T.u_q, wd(U_BX), CHIP, sem.arr_1)
     V.wait_ge(sem.ld_a0, 16)
-    quant(T.a_q, T.a_s, T.a_sb, 0, 2, sem.qa0)
+    quant(U_A, T.a_sb, 0, 2, sem.qa0)
     g.wait_ge(sem.qa0, 1)
-    send(partner, T.pa_q, T.pa_s, wd(0, 2), T.a_q, T.a_s, wd(0, 2), CHIP, sem.arr_a0)
-    V.wait_ge(sem.zz, 2)
-    for lo in (0, NT + NH):
-        V.quantize_mx(T.r_q[:, lo:lo + NT], T.r_s[:, lo:lo + NT], T.z_sb[:]).then_inc(sem.qz, 1)
+    codes(partner, T.p_q, wd(P_A, 2), T.u_q, wd(U_A, 2), CHIP, sem.arr_1)
+    plane(partner, T.p_s, wd(P_BX, 3), T.u_s, wd(U_BX, 3), CHIP, sem.arr_1)
     V.wait_ge(sem.ld_a1, 16)
-    quant(T.a_q, T.a_s, T.a_sb, 2, 2, sem.qa1)
-    g.wait_ge(sem.qa1, 1)
-    send(partner, T.pa_q, T.pa_s, wd(2, 2), T.a_q, T.a_s, wd(2, 2), SIDE, sem.arr_a1)
+    quant(U_A + 2, T.a_sb, 2, 2, sem.qa1)
     V.wait_ge(sem.ld_bm, 16)
-    quant(T.b_q, T.b_s, T.b_sb, cm, 1, sem.qbm)
+    quant(U_BM, T.b_sb, cm, 1, sem.qbm)
     V.wait_ge(sem.ld_bp, 16)
-    quant(T.b_q, T.b_s, T.b_sb, cp, 1, sem.qbp)
+    quant(U_BP, T.b_sb, cp, 1, sem.qbp)
+    g.wait_ge(sem.qa1, 1)
     g.wait_ge(sem.qbp, 1)
-    send(partner, T.pb_q, T.pb_s, wd(1), T.b_q, T.b_s, wd(cp), SIDE, sem.arr_bp)
+    codes(partner, T.p_q, wd(P_A + 2, 3), T.u_q, wd(U_A + 2, 3), SIDE, sem.arr_2)
+    plane(partner, T.p_s, wd(P_A + 2, 3), T.u_s, wd(U_A + 2, 3), SIDE, sem.arr_2)
 
     PE.wait_ge(sem.qa1, 1)
     PE.wait_ge(sem.qbx, 1)
     PE.wait_ge(sem.qbm, 1)
     for q in range(2):
-        PE.matmul_mx(bank(6 + q, 0, 2 * NT), T.a_q[:, wd(2 + q)], T.a_s[:, wd(2 + q)],
-                     T.b_q[:, wd(fl, 2)], T.b_s[:, wd(fl, 2)], True, True).then_inc(sem["ud_%d" % q], 1)
+        PE.matmul_mx(bank(6 + q, 0, 2 * NT), T.u_q[:, wd(U_A + 2 + q)], T.u_s[:, wd(U_A + 2 + q)],
+                     T.u_q[:, wd(U_BM, 2)], T.u_s[:, wd(U_BM, 2)], True, True).then_inc(sem["ud_%d" % q], 1)
     PE.wait_ge(sem.qa0, 1)
     for q in range(2):
-        mm(4 + q, T.a_q, T.a_s, q, T.b_q, T.b_s, cm, True, False)
+        mm(4 + q, T.u_q, T.u_s, U_A + q, T.u_q, T.u_s, U_BM, True, False)
     for q in range(2):
         (V if q == 0 else S).wait_ge(sem["ud_%d" % q], 1)
         for h in range(2):
-            cast(q, T.h_sb[:, 2 * h + q:NE // 2:4], bank(6 + q, NT * (cx - fl) + NH * h, NH), sem.ch)
+            cast(q, T.h_sb[:, 2 * h + q:NE // 2:4], bank(6 + q, NT + NH * h, NH), sem.ch)
+    V.wait_ge(sem.zz, 1)
     V.wait_ge(sem.ch, 4)
     V.quantize_mx(T.h_q[:], T.h_s[:], T.h_sb[:]).then_inc(sem.qh, 1)
     g.wait_ge(sem.qh, 1)
-    send(his, T.r_q, T.r_s, slice(NT, NT + NH), T.h_q, T.h_s, slice(0, NH), OUT, sem.arr_h)
+    codes(his, T.r_q, slice(NT, NT + NH), T.h_q, slice(0, NH), OUT, sem.arr_h)
+    plane(his, T.r_s, slice(NT, NT + NH), T.h_s, slice(0, NH), OUT, sem.arr_h)
     for q in range(2):
-        cast(q, T.t_sb[:, 2 + q:NE:4], bank(6 + q, NT * (cm - fl), NT), sem.ct)
+        cast(q, T.t_sb[:, 2 + q:NE:4], bank(6 + q, 0, NT), sem.ct)
     V.wait_ge(sem.ld_bo, 16)
-    quant(T.b_q, T.b_s, T.b_sb, co, 1, sem.qbo)
+    quant(U_BO, T.b_sb, co, 1, sem.qbo)
 
-    PE.wait_ge(sem.arr_bx, 2 * CHIP[1])
-    PE.wait_ge(sem.arr_a0, 2 * CHIP[1])
+    PE.wait_ge(sem.arr_1, 3 * CHIP[1])
     for q in range(2):
-        mm(4 + q, T.pa_q, T.pa_s, q, T.pb_q, T.pb_s, 0, False, True).then_inc(sem["up_%d" % q], 1)
+        mm(4 + q, T.p_q, T.p_s, P_A + q, T.p_q, T.p_s, P_BX, False, True).then_inc(sem["up_%d" % q], 1)
     for q in range(2):
         (V if q == 1 else S).wait_ge(sem["up_%d" % q], 1)
         cast(1 - q, T.t_sb[:, q:NE:4], bank(4 + q), sem.ct)
     V.wait_ge(sem.ct, 4)
     V.quantize_mx(T.t_q[:], T.t_s[:], T.t_sb[:]).then_inc(sem.qt, 1)
     g.wait_ge(sem.qt, 1)
-    send(mine, T.f_q, T.f_s, wd(0), T.t_q, T.t_s, wd(0), OUT, sem.arr_f)
+    codes(mine, T.f_q, wd(0), T.t_q, wd(0), OUT, sem.arr_f)
+    plane(mine, T.f_s, wd(0), T.t_s, wd(0), OUT, sem.arr_f)
+
+    V.wait_ge(sem.zer, 1)
+    for lo in (0, NT + NH):
+        V.quantize_mx(T.r_q[:, lo:lo + NT], T.r_s[:, lo:lo + NT], T.dia[:, 0:NE]).then_inc(sem.qz, 1)
+    V.wait_ge(sem.qz, 2)
+    V.wait_ge(sem.eye, 1)
+    V.tensor_copy(T.dia[:, 3:NE:4], T.eye[:]).then_inc(sem.dia, 1)
+    V.wait_ge(sem.dia, 1)
+    for t in range(4):
+        V.quantize_mx(T.s_q[:, wd(t)], T.s_s[:, wd(t)], T.dia[:, 3 - t:3 - t + NE]).then_inc(sem.qs, 1)
 
     PE.wait_ge(sem.qbo, 1)
     for i in range(4):
-        mm(i, T.a_q, T.a_s, i, T.b_q, T.b_s, co, True, False)
-    PE.wait_ge(sem.arr_a1, 2 * SIDE[1])
-    PE.wait_ge(sem.arr_bp, 2 * SIDE[1])
+        mm(i, T.u_q, T.u_s, U_A + i, T.u_q, T.u_s, U_BO, True, False)
+    PE.wait_ge(sem.arr_2, 2 * SIDE[1])
     for i in range(4):
-        mm(i, T.pa_q, T.pa_s, i, T.pb_q, T.pb_s, 1, False, False)
+        mm(i, T.p_q, T.p_s, P_A + i, T.p_q, T.p_s, P_BP, False, False)
     PE.wait_ge(sem.qs, 4)
     PE.wait_ge(sem.qz, 2)
     PE.wait_ge(sem.arr_h, 2 * OUT[1])

from concourse.mybir import dt, AluOpType, ActivationFunctionType

NT = 128
NH = NT // 2
NE = 4 * NT
BANK = 512

U_BM, U_BX, U_A, U_BP, U_BO = 0, 1, 2, 6, 7
P_BX, P_A, P_BP = 0, 1, 5

SCRATCH = {
    "a_sb": ("sbuf", [128, 4 * NE], "bfloat16"),
    "b_sb": ("sbuf", [128, 4 * NE], "bfloat16"),
    "u_q": ("sbuf", [128, 8 * NT], "float8_e4m3fn_x4"),
    "u_s": ("sbuf", [128, 8 * NT], "uint8"),
    "p_q": ("sbuf", [128, 6 * NT], "float8_e4m3fn_x4"),
    "p_s": ("sbuf", [128, 6 * NT], "uint8"),
    "eye": ("sbuf", [128, NT], "bfloat16"),
    "dia": ("sbuf", [128, NE + 8], "bfloat16"),
    "s_q": ("sbuf", [128, 4 * NT], "float8_e4m3fn_x4"),
    "s_s": ("sbuf", [128, 4 * NT], "uint8"),
    "t_sb": ("sbuf", [128, NE], "bfloat16"),
    "t_q": ("sbuf", [128, NT], "float8_e4m3fn_x4"),
    "t_s": ("sbuf", [128, NT], "uint8"),
    "h_sb": ("sbuf", [128, NE], "bfloat16"),
    "h_q": ("sbuf", [128, NT], "float8_e4m3fn_x4"),
    "h_s": ("sbuf", [128, NT], "uint8"),
    "f_q": ("sbuf", [128, NT], "float8_e4m3fn_x4"),
    "f_s": ("sbuf", [128, NT], "uint8"),
    "r_q": ("sbuf", [128, 2 * NT + NH], "float8_e4m3fn_x4"),
    "r_s": ("sbuf", [128, 2 * NT + NH], "uint8"),
    "y_sb": ("sbuf", [128, NE], "float32"),
    "ps": ("psum", [128, 8 * BANK], "float32"),
}

SEMAPHORES = (
    ["ld_bx", "ld_a0", "ld_a1", "ld_bm", "ld_bp", "ld_bo", "one", "zer", "zz", "eye", "dia", "qs", "qz",
     "qbx", "qa0", "qa1", "qbm", "qbp", "qbo", "ch", "ct", "c4", "qh", "qt",
     "arr_1", "arr_2", "arr_f", "arr_h", "sent", "stored"]
    + ["ud_%d" % q for q in range(2)] + ["up_%d" % q for q in range(2)] + ["uy_%d" % i for i in range(4)]
)


def _bits(mask):
    return [e for e in range(mask.bit_length()) if (mask >> e) & 1]


def _mask_of(engines):
    m = 0
    for e in engines:
        m |= 1 << e
    return m


def rank_program(g, core, T, topo):
    rank = T.rank_of(core)
    if rank is None:
        return
    V, S, PE, SY, sem = g.vector, g.scalar, g.tensor, g.sync, T.sem
    Copy = ActivationFunctionType.Copy

    others = [c for c in T.cores if c != core]
    partner = [c for c in others if topo.host(c) == topo.host(core) and topo.chip(c) == topo.chip(core)][0]
    far = [c for c in others if c != partner]
    mine = [c for c in far if topo.die(c) == topo.die(core)][0]
    his = [c for c in far if c != mine][0]
    co, cp, cm, cx = rank, T.rank_of(partner), T.rank_of(mine), T.rank_of(his)

    out_eng = _bits(topo.mask(core, mine) & topo.mask(core, his))
    chip_eng = _bits(topo.mask(core, partner))
    side_eng = [e for e in chip_eng if e not in out_eng] or chip_eng
    OUT, CHIP, SIDE = [(_mask_of(e), len(e)) for e in (out_eng, chip_eng, side_eng)]
    total = [0]

    def el(c, n=1):
        return slice(NE * c, NE * (c + n))

    def wd(c, n=1):
        return slice(NT * c, NT * (c + n))

    def bank(k, lo=0, n=NT):
        return T.ps[:, BANK * k + lo:BANK * k + lo + n]

    def mm(k, lq, ls, i, rq, rs, c, start, stop):
        return PE.matmul_mx(bank(k), lq[:, wd(i)], ls[:, wd(i)], rq[:, wd(c)], rs[:, wd(c)], start, stop)

    def codes(dst, dq, dcols, sq, scols, eng, arr):
        rid, pid = topo.addr(dst, core)
        g.remote_dma(dq[:, dcols].bitcast(dt.uint8), sq[:, scols].bitcast(dt.uint8), arr, sem.sent, pid, rid, eng[0])
        total[0] += eng[1]

    def plane(dst, ds, dcols, ss, scols, eng, arr):
        rid, pid = topo.addr(dst, core)
        g.remote_dma(ds[:, dcols], ss[:, scols], arr, sem.sent, pid, rid, eng[0])
        total[0] += eng[1]

    def quant(u, src, c, n, ready):
        V.quantize_mx(T.u_q[:, wd(u, n)], T.u_s[:, wd(u, n)], src[:, el(c, n)]).then_inc(ready, 1)

    def cast(q, out, in_, done):
        if q == 0:
            V.tensor_copy(out, in_).then_inc(done, 1)
        else:
            S.activation(out, in_, Copy).then_inc(done, 1)

    SY.dma_start(T.b_sb[:, el(cx)], T.b[:, el(cx)]).then_inc(sem.ld_bx, 16)
    S.dma_start(T.a_sb[:, el(0, 2)], T.a[:, el(0, 2)]).then_inc(sem.ld_a0, 16)
    SY.dma_start(T.a_sb[:, el(2, 2)], T.a[:, el(2, 2)]).then_inc(sem.ld_a1, 16)
    S.dma_start(T.b_sb[:, el(cm)], T.b[:, el(cm)]).then_inc(sem.ld_bm, 16)
    SY.dma_start(T.b_sb[:, el(cp)], T.b[:, el(cp)]).then_inc(sem.ld_bp, 16)
    S.dma_start(T.b_sb[:, el(co)], T.b[:, el(co)]).then_inc(sem.ld_bo, 16)

    V.memset(T.eye[:], 1.0).then_inc(sem.one, 1)
    V.memset(T.h_sb[:, NE // 2:NE], 0.0).then_inc(sem.zz, 1)
    V.memset(T.dia[:], 0.0).then_inc(sem.zer, 1)
    g.wait_ge(sem.one, 1)
    g.affine_select(T.eye[:], T.eye[:], [[-1, NT]], AluOpType.is_equal, 0.0, 0, 1).then_inc(sem.eye, 1)

    V.wait_ge(sem.ld_bx, 16)
    quant(U_BX, T.b_sb, cx, 1, sem.qbx)
    g.wait_ge(sem.qbx, 1)
    codes(partner, T.p_q, wd(P_BX), T.u_q, wd(U_BX), CHIP, sem.arr_1)
    V.wait_ge(sem.ld_a0, 16)
    quant(U_A, T.a_sb, 0, 2, sem.qa0)
    g.wait_ge(sem.qa0, 1)
    codes(partner, T.p_q, wd(P_A, 2), T.u_q, wd(U_A, 2), CHIP, sem.arr_1)
    plane(partner, T.p_s, wd(P_BX, 3), T.u_s, wd(U_BX, 3), CHIP, sem.arr_1)
    V.wait_ge(sem.ld_a1, 16)
    quant(U_A + 2, T.a_sb, 2, 2, sem.qa1)
    V.wait_ge(sem.ld_bm, 16)
    quant(U_BM, T.b_sb, cm, 1, sem.qbm)
    V.wait_ge(sem.ld_bp, 16)
    quant(U_BP, T.b_sb, cp, 1, sem.qbp)
    g.wait_ge(sem.qa1, 1)
    g.wait_ge(sem.qbp, 1)
    codes(partner, T.p_q, wd(P_A + 2, 3), T.u_q, wd(U_A + 2, 3), SIDE, sem.arr_2)
    plane(partner, T.p_s, wd(P_A + 2, 3), T.u_s, wd(U_A + 2, 3), SIDE, sem.arr_2)

    PE.wait_ge(sem.qa1, 1)
    PE.wait_ge(sem.qbx, 1)
    PE.wait_ge(sem.qbm, 1)
    for q in range(2):
        PE.matmul_mx(bank(6 + q, 0, 2 * NT), T.u_q[:, wd(U_A + 2 + q)], T.u_s[:, wd(U_A + 2 + q)],
                     T.u_q[:, wd(U_BM, 2)], T.u_s[:, wd(U_BM, 2)], True, True).then_inc(sem["ud_%d" % q], 1)
    PE.wait_ge(sem.qa0, 1)
    for q in range(2):
        mm(4 + q, T.u_q, T.u_s, U_A + q, T.u_q, T.u_s, U_BM, True, False)
    for q in range(2):
        (V if q == 0 else S).wait_ge(sem["ud_%d" % q], 1)
        for h in range(2):
            cast(q, T.h_sb[:, 2 * h + q:NE // 2:4], bank(6 + q, NT + NH * h, NH), sem.ch)
    V.wait_ge(sem.zz, 1)
    V.wait_ge(sem.ch, 4)
    V.quantize_mx(T.h_q[:], T.h_s[:], T.h_sb[:]).then_inc(sem.qh, 1)
    g.wait_ge(sem.qh, 1)
    codes(his, T.r_q, slice(NT, NT + NH), T.h_q, slice(0, NH), OUT, sem.arr_h)
    plane(his, T.r_s, slice(NT, NT + NH), T.h_s, slice(0, NH), OUT, sem.arr_h)
    for q in range(2):
        cast(q, T.t_sb[:, 2 + q:NE:4], bank(6 + q, 0, NT), sem.ct)
    V.wait_ge(sem.ld_bo, 16)
    quant(U_BO, T.b_sb, co, 1, sem.qbo)

    PE.wait_ge(sem.arr_1, 3 * CHIP[1])
    for q in range(2):
        mm(4 + q, T.p_q, T.p_s, P_A + q, T.p_q, T.p_s, P_BX, False, True).then_inc(sem["up_%d" % q], 1)
    for q in range(2):
        (V if q == 1 else S).wait_ge(sem["up_%d" % q], 1)
        cast(1 - q, T.t_sb[:, q:NE:4], bank(4 + q), sem.ct)
    V.wait_ge(sem.ct, 4)
    V.quantize_mx(T.t_q[:], T.t_s[:], T.t_sb[:]).then_inc(sem.qt, 1)
    g.wait_ge(sem.qt, 1)
    codes(mine, T.f_q, wd(0), T.t_q, wd(0), OUT, sem.arr_f)
    plane(mine, T.f_s, wd(0), T.t_s, wd(0), OUT, sem.arr_f)

    V.wait_ge(sem.zer, 1)
    for lo in (0, NT + NH):
        V.quantize_mx(T.r_q[:, lo:lo + NT], T.r_s[:, lo:lo + NT], T.dia[:, 0:NE]).then_inc(sem.qz, 1)
    V.wait_ge(sem.qz, 2)
    V.wait_ge(sem.eye, 1)
    V.tensor_copy(T.dia[:, 3:NE:4], T.eye[:]).then_inc(sem.dia, 1)
    V.wait_ge(sem.dia, 1)
    for t in range(4):
        V.quantize_mx(T.s_q[:, wd(t)], T.s_s[:, wd(t)], T.dia[:, 3 - t:3 - t + NE]).then_inc(sem.qs, 1)

    PE.wait_ge(sem.qbo, 1)
    for i in range(4):
        mm(i, T.u_q, T.u_s, U_A + i, T.u_q, T.u_s, U_BO, True, False)
    PE.wait_ge(sem.arr_2, 2 * SIDE[1])
    for i in range(4):
        mm(i, T.p_q, T.p_s, P_A + i, T.p_q, T.p_s, P_BP, False, False)
    PE.wait_ge(sem.qs, 4)
    PE.wait_ge(sem.qz, 2)
    PE.wait_ge(sem.arr_h, 2 * OUT[1])
    for q in range(2):
        for h in range(2):
            v = slice(NT - NH * h, 2 * NT - NH * h)
            PE.matmul_mx(bank(2 + q), T.s_q[:, wd(2 * h + q)], T.s_s[:, wd(2 * h + q)], T.r_q[:, v], T.r_s[:, v],
                         False, False)
    PE.wait_ge(sem.arr_f, 2 * OUT[1])
    for i in range(4):
        mm(i, T.s_q, T.s_s, i, T.f_q, T.f_s, 0, False, True).then_inc(sem["uy_%d" % i], 1)
    for i in range(4):
        (V if i % 2 == 1 else S).wait_ge(sem["uy_%d" % i], 1)
        cast(1 - i % 2, T.y_sb[:, i:NE:4], bank(i), sem.c4)
    SY.wait_ge(sem.c4, 4)
    SY.dma_start(T.y[:, :], T.y_sb[:]).then_inc(sem.stored, 16)
    SY.wait_ge(sem.stored, 16)
    g.wait_ge(sem.sent, total[0])
